import numpy as np
import ml_dtypes


def mxq(x, axis, fmt="e4m3"):
    dtype, down = {"e4m3": (ml_dtypes.float8_e4m3fn, 7), "e5m2": (ml_dtypes.float8_e5m2, 14)}[fmt]
    v = np.moveaxis(np.asarray(x, np.float32).astype(ml_dtypes.bfloat16).astype(np.float64), axis, -1)
    blocks = v.reshape(v.shape[:-1] + (-1, 32))
    amax = np.abs(blocks).max(-1, keepdims=True)
    byte = np.maximum(np.where(amax > 0, np.frexp(amax)[1] - 1 + 127, 0) - down, 1)
    scale = np.exp2(byte - 127.0)
    codes = (blocks / scale).astype(np.float32).astype(dtype).astype(np.float64)
    return np.moveaxis((codes * scale).reshape(v.shape), -1, axis)


WIDE = False


def mx_kscale(k):
    if not WIDE:
        return np.ones(k)
    levels = np.array([10, -10, 5, -5, 0])
    if k % 512:
        return np.exp2(np.random.permutation(np.resize(levels, k // 32))).repeat(32)
    a = np.empty((k // 512, 16))
    for p in range(k // 512):
        a[p, :8] = np.random.permutation(np.resize(levels, 8))
        for g in range(8):
            far = levels[np.abs(levels - a[p, g]) >= 10]
            a[p, g + 8] = far[np.random.randint(len(far))]
    return np.exp2(a.ravel()).repeat(32)


def f64(x):
    return np.asarray(x).astype(np.float64)


def striped(idx):
    return np.tile(np.asarray(idx).reshape(-1, 16).T, (8, 1)).astype(np.uint16)


def unstriped(offs):
    return offs[:16].T.reshape(-1).astype(np.int64)


E2M1 = np.array([0.0, 0.5, 1.0, 1.5, 2.0, 3.0, 4.0, 6.0, -0.0, -0.5, -1.0, -1.5, -2.0, -3.0, -4.0, -6.0])


def pack_weight(w, fmt):
    k, n = w.shape
    w = f64(np.asarray(w, np.float32).astype(ml_dtypes.bfloat16)).reshape(k // 32, 32, n)
    amax = np.abs(w).max(1)
    if fmt == "e4m3":
        byte = np.frexp(amax)[1] - 1 + 127 - 7
    else:
        mant, ex = np.frexp(amax / 6.0)
        byte = np.where(mant > 0.5, ex, ex - 1) + 127
    byte = np.clip(np.where(amax > 0, byte, 1), 1, 254)
    scaled = (w * np.exp2(127.0 - byte)[:, None, :]).reshape(k, n).astype(np.float32)
    by_word = np.ascontiguousarray(scaled.reshape(k // 512, 128, 4, n).transpose(0, 1, 3, 2))
    if fmt == "e4m3":
        words = by_word.astype(ml_dtypes.float8_e4m3fn).view(np.uint8)
    else:
        c = by_word.astype(ml_dtypes.float4_e2m1fn).view(np.uint8) & 0xF
        words = (c[..., 0::2] | (c[..., 1::2] << 4)).reshape(k // 512, 128, 2 * n)
    return np.ascontiguousarray(words), np.ascontiguousarray(byte.astype(np.uint8).reshape(k // 512, 16, n))


def unpack_weight(words, scales, fmt):
    g, _, n = scales.shape
    words = np.ascontiguousarray(words).reshape(g, 128, n, -1)
    if fmt == "e4m3":
        vals = words.view(ml_dtypes.float8_e4m3fn).astype(np.float64)
    else:
        nib = np.empty((g, 128, n, 4), np.uint8)
        nib[..., 0::2] = words & 0xF
        nib[..., 1::2] = words >> 4
        vals = E2M1[nib]
    vals = vals * np.repeat(np.exp2(scales.astype(np.float64) - 127.0), 8, axis=1)[..., None]
    return vals.transpose(0, 1, 3, 2).reshape(g * 512, n)


def bf(x):
    return np.asarray(x, np.float32).astype(ml_dtypes.bfloat16)


def planes(Y):
    r, m = Y.shape
    b = f64(bf(Y)).reshape(r // 32, 32, m)
    amax = np.abs(b).max(1)
    byte = np.clip(np.where(amax > 0, np.frexp(amax)[1] - 1 + 127 - 7, 1), 1, 254)
    codes = (b * np.exp2(127.0 - byte)[:, None, :]).reshape(r, m).astype(np.float32).astype(ml_dtypes.float8_e4m3fn).view(np.uint8)
    words = codes.reshape(r // 512, 128, 4, m).transpose(0, 1, 3, 2)
    return np.ascontiguousarray(words), np.ascontiguousarray(byte.astype(np.uint8).reshape(r // 512, 16, m))


D, T, I, J, U, X, Z, E, N = 512, 2048, 512, 512, 1024, 1024, 1024, 512, 64


def setup_inputs():
    n = np.random.standard_normal
    idx = np.random.permutation(T)[:I]
    idx2 = np.random.permutation(U)[:J]
    idx3 = np.random.permutation(X)[:I]
    idx4 = np.random.permutation(Z)[:J]
    fd = mx_kscale(D)
    fi = mx_kscale(I)
    ti = np.ones(T)
    ti[idx] = fi
    keysp = pack_weight(n((D, T)) / fd[:, None], "e2m1")
    morep = pack_weight(n((D, X)) / fd[:, None], "e2m1")
    return {
        "keys_words": keysp[0],
        "keys_scales": keysp[1],
        "notes": (n((D, U)) * 1.0 / np.sqrt(D) * fd[:, None]).astype(np.float32),
        "more_words": morep[0],
        "more_scales": morep[1],
        "users2": (n((D, Z)) * 1.0 / np.sqrt(D) * fd[:, None]).astype(np.float32),
        "rowf": (np.random.uniform(0.02, 0.08, (I, 1)) * fi[:, None]).astype(np.float32),
        "vals": (n((E, T)) / ti).astype(np.float32),
        "offs": striped(idx),
        "offs2": striped(idx2),
        "offs3": striped(idx3),
        "offs4": striped(idx4),
    }


def reference(keys_words, keys_scales, notes, more_words, more_scales, users2, rowf, vals, offs, offs2, offs3, offs4):
    idx = unstriped(offs)
    idx2 = unstriped(offs2)
    idx3 = unstriped(offs3)
    idx4 = unstriped(offs4)
    keysu = unpack_weight(keys_words, keys_scales, "e2m1")
    moreu = unpack_weight(more_words, more_scales, "e2m1")
    keysidxg = keysu[:, idx]
    notesidx2q = mxq(f64(notes)[:, idx2], 0, "e4m3")
    moreidx3g = moreu[:, idx3]
    users2idx4q = mxq(f64(users2)[:, idx4], 0, "e4m3")
    g0 = keysidxg.T @ notesidx2q + moreidx3g.T @ users2idx4q
    gr1 = g0 * f64(rowf)
    vt1 = f64(vals)[:, idx].T
    vt1q = mxq(vt1, 0, "e4m3")
    gr1q = mxq(gr1, 0, "e4m3")
    o = vt1q.T @ gr1q
    y = o.reshape(E, N, J // N).max(axis=2)
    words, scales = planes(y)
    return y, words, scales

@@ -1,0 +1,202 @@
+from contextlib import ExitStack
+
+import concourse.mybir as mybir
+from concourse.masks import make_identity
+
+F32 = mybir.dt.float32
+BF16 = mybir.dt.bfloat16
+I32 = mybir.dt.int32
+U32 = mybir.dt.uint32
+U16 = mybir.dt.uint16
+U8 = mybir.dt.uint8
+FP8X4 = mybir.dt.float8_e4m3fn_x4
+FP4X4 = mybir.dt.float4_e2m1fn_x4
+COPY = mybir.ActivationFunctionType.Copy
+
+P = 128
+PACK = 4
+SLOTS = 512
+RUN = 8
+RUNS = SLOTS // RUN
+CHUNK = 128
+CHUNKS = SLOTS // CHUNK
+
+FLOPS = 3 * 2 * 512 * 512 * 512
+
+
+def tile_attend_tab_twosum_bestruns_pl_kernel(
+    tc, keys_words, keys_scales, notes, more_words, more_scales, users2, rowf, vals,
+    offs, offs2, offs3, offs4, out_0, out_1, out_2,
+):
+    nc = tc.nc
+    with ExitStack() as ctx:
+        held = ctx.enter_context(tc.tile_pool(name="held", bufs=1))
+        psum = ctx.enter_context(tc.psum_pool(name="psum", bufs=1))
+
+        def sb(name, shape, dtype):
+            return held.tile(shape, dtype, name=name, align_bytes=64)
+
+        def load_list(name, dram):
+            tile = held.tile([P, SLOTS // 16], U16, name=name)
+            nc.sync.dma_start(tile[:], dram)
+            return tile
+
+        def load_plane(name, dram, t):
+            tile = sb(f"{name}{t}", [P, dram.shape[1]], F32)
+            nc.sync.dma_start(tile[:], dram.rearrange("(p t) c -> t p c", t=PACK)[t])
+            return tile
+
+        def load_words(name, dram):
+            tile = sb(name, [P, dram.shape[2] // 2], U16)
+            nc.sync.dma_start(tile[:].bitcast(I32), dram[0].bitcast(I32))
+            return tile
+
+        def load_scale_rows(name, dram):
+            tile = sb(name, [P, dram.shape[2]], U8)
+            nc.vector.memset(tile[:].bitcast(I32), 0)
+            for q in range(4):
+                nc.gpsimd.dma_start(
+                    tile[32 * q : 32 * q + 4, :].bitcast(I32), dram[0, 4 * q : 4 * q + 4, :].bitcast(I32)
+                )
+            return tile
+
+        keys_scale_pool = load_scale_rows("keys_scale_pool", keys_scales)
+        more_scale_pool = load_scale_rows("more_scale_pool", more_scales)
+
+        note_list = load_list("note_list", offs2)
+        note_planes = [load_plane("note_plane", notes, 0)]
+        token_list = load_list("token_list", offs)
+        keys_pool = load_words("keys_pool", keys_words)
+        note_planes += [load_plane("note_plane", notes, t) for t in range(1, PACK)]
+        more_list = load_list("more_list", offs3)
+        more_pool = load_words("more_pool", more_words)
+        user_list = load_list("user_list", offs4)
+        user_planes = [load_plane("user_plane", users2, t) for t in range(PACK)]
+        row_factor = sb("row_factor", [P, PACK], F32)
+        nc.sync.dma_start(row_factor[:], rowf.rearrange("(p t) o -> p (t o)", t=PACK))
+        value_planes = [load_plane("value_plane", vals, t) for t in range(PACK)]
+
+        identity = sb("identity", [P, P], F32)
+        make_identity(nc, identity[:])
+
+        def gather_packed(name, words_pool, scale_pool, offsets):
+            words = sb(f"{name}_words", [P, SLOTS], U16)
+            nc.vector.tensor_copy(words[:], words_pool[:].indirect(offsets[:]))
+            dealt = sb(f"{name}_dealt", [P, SLOTS], U16)
+            nc.vector.tensor_copy(
+                dealt[:].rearrange("p (r s) -> p r s", r=PACK), words[:].rearrange("p (s r) -> p r s", r=PACK)
+            )
+            scales = sb(f"{name}_scales", [P, SLOTS], U8)
+            nc.vector.tensor_copy(
+                scales[:].rearrange("p (r s) -> p s r", r=PACK), scale_pool[:].indirect(offsets[:])
+            )
+            return dealt, scales
+
+        def gather_planes(name, planes, offsets):
+            picked = sb(f"{name}_picked", [P, PACK, SLOTS], BF16)
+            for t in range(PACK):
+                nc.scalar.activation(picked[:, t, :], planes[t][:].indirect(offsets[:]), COPY)
+            return picked
+
+        def weave(name, picked, c):
+            woven = sb(f"{name}_woven{c}", [P, CHUNK, PACK], BF16)
+            nc.vector.tensor_copy(
+                woven[:], picked[:, :, c * CHUNK : (c + 1) * CHUNK].rearrange("p t j -> p j t")
+            )
+            return woven
+
+        def quantize(name, woven, width):
+            codes = sb(f"{name}_codes", [P, width], U32)
+            scales = sb(f"{name}_scales", [P, width], U8)
+            nc.vector.quantize_mx(
+                out=codes[:].bitcast(FP8X4), scales=scales[:], in_=woven[:].rearrange("p j t -> p (j t)")
+            )
+            return codes, scales
+
+        keys_dealt, keys_dealt_scales = gather_packed("keys", keys_pool, keys_scale_pool, token_list)
+        notes_picked = gather_planes("notes", note_planes, note_list)
+        more_dealt, more_dealt_scales = gather_packed("more", more_pool, more_scale_pool, more_list)
+        users_picked = gather_planes("users", user_planes, user_list)
+
+        notes_woven = [weave("notes", notes_picked, c) for c in range(CHUNKS)]
+        notes_q = [quantize(f"notes{c}", notes_woven[c], CHUNK) for c in range(CHUNKS)]
+        users_woven = [weave("users", users_picked, c) for c in range(CHUNKS)]
+        users_q = [quantize(f"users{c}", users_woven[c], CHUNK) for c in range(CHUNKS)]
+
+        table_codes = sb("table_codes", [P, SLOTS], U32)
+        table_scales = sb("table_scales", [P, SLOTS], U8)
+        factor = row_factor[:].unsqueeze(1).to_broadcast([P, CHUNK, PACK])
+        table_woven = []
+        for c in range(CHUNKS):
+            bank = psum.tile([P, PACK, CHUNK], F32, name=f"table_bank{c}")
+            for t in range(PACK):
+                rows = slice(t * P, (t + 1) * P)
+                for words, scales, moving, first in (
+                    (keys_dealt, keys_dealt_scales, notes_q[c], True),
+                    (more_dealt, more_dealt_scales, users_q[c], False),
+                ):
+                    nc.tensor.matmul_mx(
+                        out=bank[:, t, :],
+                        lhsT=words[:, rows].bitcast(FP4X4),
+                        lhsT_scale=scales[:, rows],
+                        rhs=moving[0][:].bitcast(FP8X4),
+                        rhs_scale=moving[1][:],
+                        start=first,
+                        stop=not first,
+                    )
+            woven = sb(f"table_woven{c}", [P, CHUNK, PACK], BF16)
+            nc.vector.tensor_tensor(
+                woven[:], bank[:].rearrange("p t j -> p j t"), factor, mybir.AluOpType.mult
+            )
+            table_woven.append(woven)
+        for c in range(CHUNKS):
+            cols = slice(c * CHUNK, (c + 1) * CHUNK)
+            nc.vector.quantize_mx(
+                out=table_codes[:, cols].bitcast(FP8X4),
+                scales=table_scales[:, cols],
+                in_=table_woven[c][:].rearrange("p j t -> p (j t)"),
+            )
+
+        best = sb("best", [P, PACK, RUNS], F32)
+        for t in range(PACK):
+            picked = sb(f"values_picked{t}", [P, SLOTS], BF16)
+            nc.scalar.activation(picked[:], value_planes[t][:].indirect(token_list[:]), COPY)
+            pairs = picked[:].bitcast(F32)
+            turned = psum.tile([P, 2, P], F32, name=f"turned{t % 2}")
+            for u in range(2):
+                nc.tensor.transpose(turned[:, u, :], pairs[:, u::2], identity[:])
+            woven = sb(f"values_woven{t}", [P, P, PACK], BF16)
+            nc.scalar.copy(
+                woven[:].rearrange("p e t -> p (e t)").bitcast(F32).rearrange("p (e u) -> p e u", u=2),
+                turned[:].rearrange("p u e -> p e u"),
+            )
+            codes, scales = quantize(f"values{t}", woven, P)
+            sums = psum.tile([P, SLOTS], F32, name=f"sums{t % 2}")
+            nc.tensor.matmul_mx(
+                out=sums[:],
+                lhsT=codes[:].bitcast(FP8X4),
+                lhsT_scale=scales[:],
+                rhs=table_codes[:].bitcast(FP8X4),
+                rhs_scale=table_scales[:],
+                start=True,
+                stop=True,
+            )
+            nc.vector.tensor_reduce(
+                best[:, t, :],
+                sums[:].rearrange("p (n k) -> p n k", k=RUN),
+                mybir.AxisListType.X,
+                mybir.AluOpType.max,
+            )
+
+        nc.sync.dma_start(out_0.rearrange("(p t) n -> p t n", t=PACK), best[:])
+        best_woven = sb("best_woven", [P, RUNS, PACK], BF16)
+        nc.vector.tensor_copy(best_woven[:], best[:].rearrange("p t n -> p n t"))
+        best_codes, best_scales = quantize("best", best_woven, RUNS)
+        nc.sync.dma_start(
+            out_1[0].rearrange("p c r -> p (c r)").bitcast(I32), best_codes[:].bitcast(I32)
+        )
+        for q in range(4):
+            queue = nc.scalar if q % 2 == 0 else nc.sync
+            queue.dma_start(
+                out_2[0, 4 * q : 4 * q + 4, :].bitcast(I32), best_scales[32 * q : 32 * q + 4, :].bitcast(I32)
+            )

@@ -20,6 +20,7 @@ RUN = 8
 RUNS = SLOTS // RUN
 CHUNK = 128
 CHUNKS = SLOTS // CHUNK
+HALF = SLOTS // 2
 
 FLOPS = 3 * 2 * 512 * 512 * 512
 
@@ -51,27 +52,41 @@ def tile_attend_tab_twosum_bestruns_pl_kernel(
             nc.sync.dma_start(tile[:].bitcast(I32), dram[0].bitcast(I32))
             return tile
 
-        def load_scale_rows(name, dram):
-            tile = sb(name, [P, dram.shape[2]], U8)
-            nc.vector.memset(tile[:].bitcast(I32), 0)
-            for q in range(4):
-                nc.gpsimd.dma_start(
-                    tile[32 * q : 32 * q + 4, :].bitcast(I32), dram[0, 4 * q : 4 * q + 4, :].bitcast(I32)
-                )
+        def zeroed(name, width, engine):
+            tile = sb(name, [P, width], U8)
+            engine.memset(tile[:].bitcast(I32), 0)
             return tile
 
-        keys_scale_pool = load_scale_rows("keys_scale_pool", keys_scales)
-        more_scale_pool = load_scale_rows("more_scale_pool", more_scales)
+        def load_scale_rows(tile, dram, q):
+            nc.sync.dma_start(
+                tile[32 * q : 32 * q + 4, :].bitcast(I32), dram[0, 4 * q : 4 * q + 4, :].bitcast(I32)
+            )
 
-        note_list = load_list("note_list", offs2)
-        note_planes = [load_plane("note_plane", notes, 0)]
+        keys_scale_pool = zeroed("keys_scale_pool", keys_scales.shape[2], nc.gpsimd)
+        more_scale_pool = zeroed("more_scale_pool", more_scales.shape[2], nc.gpsimd)
+
         token_list = load_list("token_list", offs)
         keys_pool = load_words("keys_pool", keys_words)
-        note_planes += [load_plane("note_plane", notes, t) for t in range(1, PACK)]
+        note_list = load_list("note_list", offs2)
+        note_planes = [load_plane("note_plane", notes, 0)]
+        load_scale_rows(keys_scale_pool, keys_scales, 0)
+        note_planes.append(load_plane("note_plane", notes, 1))
+        load_scale_rows(keys_scale_pool, keys_scales, 1)
+        load_scale_rows(keys_scale_pool, keys_scales, 2)
+        note_planes.append(load_plane("note_plane", notes, 2))
+        load_scale_rows(keys_scale_pool, keys_scales, 3)
+        note_planes.append(load_plane("note_plane", notes, 3))
         more_list = load_list("more_list", offs3)
         more_pool = load_words("more_pool", more_words)
         user_list = load_list("user_list", offs4)
-        user_planes = [load_plane("user_plane", users2, t) for t in range(PACK)]
+        user_planes = [load_plane("user_plane", users2, 0)]
+        load_scale_rows(more_scale_pool, more_scales, 0)
+        user_planes.append(load_plane("user_plane", users2, 1))
+        load_scale_rows(more_scale_pool, more_scales, 1)
+        load_scale_rows(more_scale_pool, more_scales, 2)
+        user_planes.append(load_plane("user_plane", users2, 2))
+        load_scale_rows(more_scale_pool, more_scales, 3)
+        user_planes.append(load_plane("user_plane", users2, 3))
         row_factor = sb("row_factor", [P, PACK], F32)
         nc.sync.dma_start(row_factor[:], rowf.rearrange("(p t) o -> p (t o)", t=PACK))
         value_planes = [load_plane("value_plane", vals, t) for t in range(PACK)]
@@ -92,17 +107,12 @@ def tile_attend_tab_twosum_bestruns_pl_kernel(
             )
             return dealt, scales
 
-        def gather_planes(name, planes, offsets):
-            picked = sb(f"{name}_picked", [P, PACK, SLOTS], BF16)
-            for t in range(PACK):
-                nc.scalar.activation(picked[:, t, :], planes[t][:].indirect(offsets[:]), COPY)
-            return picked
+        def half_of(offsets, h):
+            return offsets[:, h * 16 : (h + 1) * 16]
 
-        def weave(name, picked, c):
-            woven = sb(f"{name}_woven{c}", [P, CHUNK, PACK], BF16)
-            nc.vector.tensor_copy(
-                woven[:], picked[:, :, c * CHUNK : (c + 1) * CHUNK].rearrange("p t j -> p j t")
-            )
+        def weave(name, picked):
+            woven = sb(name, [P, picked.shape[2], PACK], BF16)
+            nc.vector.tensor_copy(woven[:], picked.rearrange("p t j -> p j t"))
             return woven
 
         def quantize(name, woven, width):
@@ -114,55 +124,52 @@ def tile_attend_tab_twosum_bestruns_pl_kernel(
             return codes, scales
 
         keys_dealt, keys_dealt_scales = gather_packed("keys", keys_pool, keys_scale_pool, token_list)
-        notes_picked = gather_planes("notes", note_planes, note_list)
         more_dealt, more_dealt_scales = gather_packed("more", more_pool, more_scale_pool, more_list)
-        users_picked = gather_planes("users", user_planes, user_list)
 
-        notes_woven = [weave("notes", notes_picked, c) for c in range(CHUNKS)]
-        notes_q = [quantize(f"notes{c}", notes_woven[c], CHUNK) for c in range(CHUNKS)]
-        users_woven = [weave("users", users_picked, c) for c in range(CHUNKS)]
-        users_q = [quantize(f"users{c}", users_woven[c], CHUNK) for c in range(CHUNKS)]
+        notes_picked = sb("notes_picked", [P, PACK, SLOTS], BF16)
+        for t in (0, 2, 3):
+            nc.scalar.activation(notes_picked[:, t, :], note_planes[t][:].indirect(note_list[:]), COPY)
+        nc.vector.tensor_copy(notes_picked[:, 1, :], note_planes[1][:].indirect(note_list[:]))
+        users_picked = sb("users_picked", [P, PACK, SLOTS], BF16)
+        for t in range(2):
+            nc.scalar.activation(users_picked[:, t, :], user_planes[t][:].indirect(user_list[:]), COPY)
+        for t, h in ((2, 0), (2, 1), (3, 1)):
+            nc.scalar.activation(
+                users_picked[:, t, h * HALF : (h + 1) * HALF],
+                user_planes[t][:].indirect(half_of(user_list, h)),
+                COPY,
+            )
+        notes_codes, notes_scales = quantize("notes", weave("notes_woven", notes_picked[:]), SLOTS)
+        nc.vector.tensor_copy(users_picked[:, 3, :HALF], user_planes[3][:].indirect(half_of(user_list, 0)))
 
-        table_codes = sb("table_codes", [P, SLOTS], U32)
-        table_scales = sb("table_scales", [P, SLOTS], U8)
-        factor = row_factor[:].unsqueeze(1).to_broadcast([P, CHUNK, PACK])
-        table_woven = []
-        for c in range(CHUNKS):
-            bank = psum.tile([P, PACK, CHUNK], F32, name=f"table_bank{c}")
+        banks = [psum.tile([P, PACK, CHUNK], F32, name=f"bank{c}") for c in range(CHUNKS)]
+
+        def table_passes(c, words, scales, moving_codes, moving_scales, opens):
             for t in range(PACK):
                 rows = slice(t * P, (t + 1) * P)
-                for words, scales, moving, first in (
-                    (keys_dealt, keys_dealt_scales, notes_q[c], True),
-                    (more_dealt, more_dealt_scales, users_q[c], False),
-                ):
-                    nc.tensor.matmul_mx(
-                        out=bank[:, t, :],
-                        lhsT=words[:, rows].bitcast(FP4X4),
-                        lhsT_scale=scales[:, rows],
-                        rhs=moving[0][:].bitcast(FP8X4),
-                        rhs_scale=moving[1][:],
-                        start=first,
-                        stop=not first,
-                    )
-            woven = sb(f"table_woven{c}", [P, CHUNK, PACK], BF16)
-            nc.vector.tensor_tensor(
-                woven[:], bank[:].rearrange("p t j -> p j t"), factor, mybir.AluOpType.mult
-            )
-            table_woven.append(woven)
+                nc.tensor.matmul_mx(
+                    out=banks[c][:, t, :],
+                    lhsT=words[:, rows].bitcast(FP4X4),
+                    lhsT_scale=scales[:, rows],
+                    rhs=moving_codes.bitcast(FP8X4),
+                    rhs_scale=moving_scales,
+                    start=opens and t == 0,
+                    stop=not opens and t == PACK - 1,
+                )
+
         for c in range(CHUNKS):
             cols = slice(c * CHUNK, (c + 1) * CHUNK)
-            nc.vector.quantize_mx(
-                out=table_codes[:, cols].bitcast(FP8X4),
-                scales=table_scales[:, cols],
-                in_=table_woven[c][:].rearrange("p j t -> p (j t)"),
-            )
+            table_passes(c, keys_dealt, keys_dealt_scales, notes_codes[:, cols], notes_scales[:, cols], True)
 
-        best = sb("best", [P, PACK, RUNS], F32)
-        for t in range(PACK):
+        def turn(t):
             picked = sb(f"values_picked{t}", [P, SLOTS], BF16)
-            nc.scalar.activation(picked[:], value_planes[t][:].indirect(token_list[:]), COPY)
+            if t + 1 < PACK:
+                nc.scalar.activation(picked[:], value_planes[t][:].indirect(token_list[:]), COPY)
+            else:
+                nc.scalar.activation(picked[:, :HALF], value_planes[t][:].indirect(half_of(token_list, 0)), COPY)
+                nc.vector.tensor_copy(picked[:, HALF:], value_planes[t][:].indirect(half_of(token_list, 1)))
             pairs = picked[:].bitcast(F32)
-            turned = psum.tile([P, 2, P], F32, name=f"turned{t % 2}")
+            turned = psum.tile([P, 2, P], F32, name=f"turned{t}")
             for u in range(2):
                 nc.tensor.transpose(turned[:, u, :], pairs[:, u::2], identity[:])
             woven = sb(f"values_woven{t}", [P, P, PACK], BF16)
@@ -170,8 +177,41 @@ def tile_attend_tab_twosum_bestruns_pl_kernel(
                 woven[:].rearrange("p e t -> p (e t)").bitcast(F32).rearrange("p (e u) -> p e u", u=2),
                 turned[:].rearrange("p u e -> p e u"),
             )
+            return woven
+
+        values_woven = [turn(0)]
+
+        table_codes = sb("table_codes", [P, SLOTS], U32)
+        table_scales = sb("table_scales", [P, SLOTS], U8)
+        factor = row_factor[:].unsqueeze(1).to_broadcast([P, CHUNK, PACK])
+        users_woven = [
+            weave(f"users_woven{h}", users_picked[:, :, h * HALF : (h + 1) * HALF]) for h in range(2)
+        ]
+        table_woven = [sb(f"table_woven{h}", [P, HALF, PACK], BF16) for h in range(2)]
+        for h in range(2):
+            codes, scales = quantize(f"users{h}", users_woven[h], HALF)
+            for k in range(2):
+                cols = slice(k * CHUNK, (k + 1) * CHUNK)
+                table_passes(2 * h + k, more_dealt, more_dealt_scales, codes[:, cols], scales[:, cols], False)
+        for h in range(2):
+            for k in range(2):
+                nc.vector.tensor_tensor(
+                    table_woven[h][:, k * CHUNK : (k + 1) * CHUNK, :],
+                    banks[2 * h + k][:].rearrange("p t j -> p j t"),
+                    factor,
+                    mybir.AluOpType.mult,
+                )
+        for h in range(2):
+            cols = slice(h * HALF, (h + 1) * HALF)
+            nc.vector.quantize_mx(
+                out=table_codes[:, cols].bitcast(FP8X4),
+                scales=table_scales[:, cols],
+                in_=table_woven[h][:].rearrange("p j t -> p (j t)"),
+            )
+
+        def multiply(t, woven):
             codes, scales = quantize(f"values{t}", woven, P)
-            sums = psum.tile([P, SLOTS], F32, name=f"sums{t % 2}")
+            sums = psum.tile([P, SLOTS], F32, name="turned1" if t == 0 else f"bank{t}")
             nc.tensor.matmul_mx(
                 out=sums[:],
                 lhsT=codes[:].bitcast(FP8X4),
@@ -181,16 +221,28 @@ def tile_attend_tab_twosum_bestruns_pl_kernel(
                 start=True,
                 stop=True,
             )
+            return sums
+
+        def best_of_runs(best, sums):
             nc.vector.tensor_reduce(
-                best[:, t, :],
-                sums[:].rearrange("p (n k) -> p n k", k=RUN),
-                mybir.AxisListType.X,
-                mybir.AluOpType.max,
+                best, sums[:].rearrange("p (n k) -> p n k", k=RUN), mybir.AxisListType.X, mybir.AluOpType.max
             )
 
-        nc.sync.dma_start(out_0.rearrange("(p t) n -> p t n", t=PACK), best[:])
-        best_woven = sb("best_woven", [P, RUNS, PACK], BF16)
-        nc.vector.tensor_copy(best_woven[:], best[:].rearrange("p t n -> p n t"))
+        out_pairs = out_0.rearrange("(p u e) n -> u p e n", u=2, e=2)
+        values_woven.append(turn(1))
+        best_low = sb("best_low", [P, 2, RUNS], F32)
+        for t in range(2):
+            best_of_runs(best_low[:, t, :], multiply(t, values_woven[t]))
+        nc.sync.dma_start(out_pairs[0], best_low[:])
+        sums = [multiply(t, turn(t)) for t in range(2, PACK)]
+        best_high = sb("value_plane3", [P, 2, RUNS], F32)
+        for e in range(2):
+            best_of_runs(best_high[:, e, :], sums[e])
+        nc.sync.dma_start(out_pairs[1], best_high[:])
+
+        best_woven = sb("values_picked3", [P, RUNS, PACK], BF16)
+        for u, best in enumerate((best_low, best_high)):
+            nc.scalar.copy(best_woven[:, :, 2 * u : 2 * u + 2], best[:].rearrange("p e n -> p n e"))
         best_codes, best_scales = quantize("best", best_woven, RUNS)
         nc.sync.dma_start(
             out_1[0].rearrange("p c r -> p (c r)").bitcast(I32), best_codes[:].bitcast(I32)

@@ -52,9 +52,9 @@ def tile_attend_tab_twosum_bestruns_pl_kernel(
             nc.sync.dma_start(tile[:].bitcast(I32), dram[0].bitcast(I32))
             return tile
 
-        def zeroed(name, width, engine):
+        def zeroed(name, width):
             tile = sb(name, [P, width], U8)
-            engine.memset(tile[:].bitcast(I32), 0)
+            nc.gpsimd.memset(tile[:].bitcast(I32), 0)
             return tile
 
         def load_scale_rows(tile, dram, q):
@@ -62,31 +62,28 @@ def tile_attend_tab_twosum_bestruns_pl_kernel(
                 tile[32 * q : 32 * q + 4, :].bitcast(I32), dram[0, 4 * q : 4 * q + 4, :].bitcast(I32)
             )
 
-        keys_scale_pool = zeroed("keys_scale_pool", keys_scales.shape[2], nc.gpsimd)
-        more_scale_pool = zeroed("more_scale_pool", more_scales.shape[2], nc.gpsimd)
+        keys_scale_pool = zeroed("keys_scale_pool", keys_scales.shape[2])
+        more_scale_pool = zeroed("more_scale_pool", more_scales.shape[2])
 
         token_list = load_list("token_list", offs)
         keys_pool = load_words("keys_pool", keys_words)
+        load_scale_rows(keys_scale_pool, keys_scales, 0)
         note_list = load_list("note_list", offs2)
         note_planes = [load_plane("note_plane", notes, 0)]
-        load_scale_rows(keys_scale_pool, keys_scales, 0)
-        note_planes.append(load_plane("note_plane", notes, 1))
         load_scale_rows(keys_scale_pool, keys_scales, 1)
         load_scale_rows(keys_scale_pool, keys_scales, 2)
-        note_planes.append(load_plane("note_plane", notes, 2))
+        note_planes.append(load_plane("note_plane", notes, 1))
         load_scale_rows(keys_scale_pool, keys_scales, 3)
-        note_planes.append(load_plane("note_plane", notes, 3))
         more_list = load_list("more_list", offs3)
         more_pool = load_words("more_pool", more_words)
-        user_list = load_list("user_list", offs4)
-        user_planes = [load_plane("user_plane", users2, 0)]
+        note_planes.append(load_plane("note_plane", notes, 2))
         load_scale_rows(more_scale_pool, more_scales, 0)
-        user_planes.append(load_plane("user_plane", users2, 1))
         load_scale_rows(more_scale_pool, more_scales, 1)
+        note_planes.append(load_plane("note_plane", notes, 3))
         load_scale_rows(more_scale_pool, more_scales, 2)
-        user_planes.append(load_plane("user_plane", users2, 2))
         load_scale_rows(more_scale_pool, more_scales, 3)
-        user_planes.append(load_plane("user_plane", users2, 3))
+        user_list = load_list("user_list", offs4)
+        user_planes = [load_plane("user_plane", users2, t) for t in range(PACK)]
         row_factor = sb("row_factor", [P, PACK], F32)
         nc.sync.dma_start(row_factor[:], rowf.rearrange("(p t) o -> p (t o)", t=PACK))
         value_planes = [load_plane("value_plane", vals, t) for t in range(PACK)]
@@ -94,18 +91,19 @@ def tile_attend_tab_twosum_bestruns_pl_kernel(
         identity = sb("identity", [P, P], F32)
         make_identity(nc, identity[:])
 
-        def gather_packed(name, words_pool, scale_pool, offsets):
+        def gather_words(name, pool, offsets):
             words = sb(f"{name}_words", [P, SLOTS], U16)
-            nc.vector.tensor_copy(words[:], words_pool[:].indirect(offsets[:]))
+            nc.vector.tensor_copy(words[:], pool[:].indirect(offsets[:]))
             dealt = sb(f"{name}_dealt", [P, SLOTS], U16)
             nc.vector.tensor_copy(
                 dealt[:].rearrange("p (r s) -> p r s", r=PACK), words[:].rearrange("p (s r) -> p r s", r=PACK)
             )
+            return dealt
+
+        def gather_scales(name, pool, offsets):
             scales = sb(f"{name}_scales", [P, SLOTS], U8)
-            nc.vector.tensor_copy(
-                scales[:].rearrange("p (r s) -> p s r", r=PACK), scale_pool[:].indirect(offsets[:])
-            )
-            return dealt, scales
+            nc.vector.tensor_copy(scales[:].rearrange("p (r s) -> p s r", r=PACK), pool[:].indirect(offsets[:]))
+            return scales
 
         def half_of(offsets, h):
             return offsets[:, h * 16 : (h + 1) * 16]
@@ -123,14 +121,17 @@ def tile_attend_tab_twosum_bestruns_pl_kernel(
             )
             return codes, scales
 
-        keys_dealt, keys_dealt_scales = gather_packed("keys", keys_pool, keys_scale_pool, token_list)
-        more_dealt, more_dealt_scales = gather_packed("more", more_pool, more_scale_pool, more_list)
-
         notes_picked = sb("notes_picked", [P, PACK, SLOTS], BF16)
-        for t in (0, 2, 3):
-            nc.scalar.activation(notes_picked[:, t, :], note_planes[t][:].indirect(note_list[:]), COPY)
-        nc.vector.tensor_copy(notes_picked[:, 1, :], note_planes[1][:].indirect(note_list[:]))
         users_picked = sb("users_picked", [P, PACK, SLOTS], BF16)
+        keys_dealt = gather_words("keys", keys_pool, token_list)
+        keys_dealt_scales = gather_scales("keys", keys_scale_pool, token_list)
+        more_dealt = gather_words("more", more_pool, more_list)
+        for t in range(PACK - 1):
+            nc.scalar.activation(notes_picked[:, t, :], note_planes[t][:].indirect(note_list[:]), COPY)
+        nc.vector.tensor_copy(notes_picked[:, PACK - 1, :], note_planes[PACK - 1][:].indirect(note_list[:]))
+        more_dealt_scales = gather_scales("more", more_scale_pool, more_list)
+        notes_codes, notes_scales = quantize("notes", weave("notes_woven", notes_picked[:]), SLOTS)
+
         for t in range(2):
             nc.scalar.activation(users_picked[:, t, :], user_planes[t][:].indirect(user_list[:]), COPY)
         for t, h in ((2, 0), (2, 1), (3, 1)):
@@ -139,7 +140,6 @@ def tile_attend_tab_twosum_bestruns_pl_kernel(
                 user_planes[t][:].indirect(half_of(user_list, h)),
                 COPY,
             )
-        notes_codes, notes_scales = quantize("notes", weave("notes_woven", notes_picked[:]), SLOTS)
         nc.vector.tensor_copy(users_picked[:, 3, :HALF], user_planes[3][:].indirect(half_of(user_list, 0)))
 
         banks = [psum.tile([P, PACK, CHUNK], F32, name=f"bank{c}") for c in range(CHUNKS)]
@@ -161,35 +161,13 @@ def tile_attend_tab_twosum_bestruns_pl_kernel(
             cols = slice(c * CHUNK, (c + 1) * CHUNK)
             table_passes(c, keys_dealt, keys_dealt_scales, notes_codes[:, cols], notes_scales[:, cols], True)
 
-        def turn(t):
-            picked = sb(f"values_picked{t}", [P, SLOTS], BF16)
-            if t + 1 < PACK:
-                nc.scalar.activation(picked[:], value_planes[t][:].indirect(token_list[:]), COPY)
-            else:
-                nc.scalar.activation(picked[:, :HALF], value_planes[t][:].indirect(half_of(token_list, 0)), COPY)
-                nc.vector.tensor_copy(picked[:, HALF:], value_planes[t][:].indirect(half_of(token_list, 1)))
-            pairs = picked[:].bitcast(F32)
-            turned = psum.tile([P, 2, P], F32, name=f"turned{t}")
-            for u in range(2):
-                nc.tensor.transpose(turned[:, u, :], pairs[:, u::2], identity[:])
-            woven = sb(f"values_woven{t}", [P, P, PACK], BF16)
-            nc.scalar.copy(
-                woven[:].rearrange("p e t -> p (e t)").bitcast(F32).rearrange("p (e u) -> p e u", u=2),
-                turned[:].rearrange("p u e -> p e u"),
-            )
-            return woven
-
-        values_woven = [turn(0)]
-
         table_codes = sb("table_codes", [P, SLOTS], U32)
         table_scales = sb("table_scales", [P, SLOTS], U8)
         factor = row_factor[:].unsqueeze(1).to_broadcast([P, CHUNK, PACK])
-        users_woven = [
-            weave(f"users_woven{h}", users_picked[:, :, h * HALF : (h + 1) * HALF]) for h in range(2)
-        ]
         table_woven = [sb(f"table_woven{h}", [P, HALF, PACK], BF16) for h in range(2)]
         for h in range(2):
-            codes, scales = quantize(f"users{h}", users_woven[h], HALF)
+            users_woven = weave(f"users_woven{h}", users_picked[:, :, h * HALF : (h + 1) * HALF])
+            codes, scales = quantize(f"users{h}", users_woven, HALF)
             for k in range(2):
                 cols = slice(k * CHUNK, (k + 1) * CHUNK)
                 table_passes(2 * h + k, more_dealt, more_dealt_scales, codes[:, cols], scales[:, cols], False)
@@ -209,9 +187,30 @@ def tile_attend_tab_twosum_bestruns_pl_kernel(
                 in_=table_woven[h][:].rearrange("p j t -> p (j t)"),
             )
 
-        def multiply(t, woven):
+        def pick_and_turn(t):
+            picked = sb(f"values_picked{t}", [P, SLOTS], BF16)
+            if t + 1 < PACK:
+                nc.scalar.activation(picked[:], value_planes[t][:].indirect(token_list[:]), COPY)
+            else:
+                nc.scalar.activation(picked[:, :HALF], value_planes[t][:].indirect(half_of(token_list, 0)), COPY)
+                nc.vector.tensor_copy(picked[:, HALF:], value_planes[t][:].indirect(half_of(token_list, 1)))
+            pairs = picked[:].bitcast(F32)
+            turned = psum.tile([P, 2, P], F32, name=f"turned{t}")
+            for u in range(2):
+                nc.tensor.transpose(turned[:, u, :], pairs[:, u::2], identity[:])
+            return turned
+
+        def weave_turned(slot, turned):
+            woven = sb(slot, [P, P, PACK], BF16)
+            nc.scalar.copy(
+                woven[:].rearrange("p e t -> p (e t)").bitcast(F32).rearrange("p (e u) -> p e u", u=2),
+                turned[:].rearrange("p u e -> p e u"),
+            )
+            return woven
+
+        def multiply(t, woven, bank):
             codes, scales = quantize(f"values{t}", woven, P)
-            sums = psum.tile([P, SLOTS], F32, name="turned1" if t == 0 else f"bank{t}")
+            sums = psum.tile([P, SLOTS], F32, name=bank)
             nc.tensor.matmul_mx(
                 out=sums[:],
                 lhsT=codes[:].bitcast(FP8X4),
@@ -229,19 +228,20 @@ def tile_attend_tab_twosum_bestruns_pl_kernel(
             )
 
         out_pairs = out_0.rearrange("(p u e) n -> u p e n", u=2, e=2)
-        values_woven.append(turn(1))
-        best_low = sb("best_low", [P, 2, RUNS], F32)
-        for t in range(2):
-            best_of_runs(best_low[:, t, :], multiply(t, values_woven[t]))
-        nc.sync.dma_start(out_pairs[0], best_low[:])
-        sums = [multiply(t, turn(t)) for t in range(2, PACK)]
-        best_high = sb("value_plane3", [P, 2, RUNS], F32)
-        for e in range(2):
-            best_of_runs(best_high[:, e, :], sums[e])
-        nc.sync.dma_start(out_pairs[1], best_high[:])
+        best_pairs = []
+        for u in range(2):
+            even, odd = 2 * u, 2 * u + 1
+            turned = [pick_and_turn(even), pick_and_turn(odd)]
+            woven = [weave_turned(f"value_plane{odd}", turned[0]), weave_turned(f"values_woven{odd}", turned[1])]
+            sums = [multiply(2 * u + e, woven[e], f"bank{2 * u + e}") for e in range(2)]
+            best = sb(f"best{u}", [P, 2, RUNS], F32)
+            for e in range(2):
+                best_of_runs(best[:, e, :], sums[e])
+            nc.sync.dma_start(out_pairs[u], best[:])
+            best_pairs.append(best)
 
         best_woven = sb("values_picked3", [P, RUNS, PACK], BF16)
-        for u, best in enumerate((best_low, best_high)):
+        for u, best in enumerate(best_pairs):
             nc.scalar.copy(best_woven[:, :, 2 * u : 2 * u + 2], best[:].rearrange("p e n -> p n e"))
         best_codes, best_scales = quantize("best", best_woven, RUNS)
         nc.sync.dma_start(

from contextlib import ExitStack

import concourse.mybir as mybir
from concourse.masks import make_identity

F32 = mybir.dt.float32
BF16 = mybir.dt.bfloat16
I32 = mybir.dt.int32
U32 = mybir.dt.uint32
U16 = mybir.dt.uint16
U8 = mybir.dt.uint8
FP8X4 = mybir.dt.float8_e4m3fn_x4
FP4X4 = mybir.dt.float4_e2m1fn_x4
COPY = mybir.ActivationFunctionType.Copy

P = 128
PACK = 4
SLOTS = 512
RUN = 8
RUNS = SLOTS // RUN
CHUNK = 128
CHUNKS = SLOTS // CHUNK
HALF = SLOTS // 2

FLOPS = 3 * 2 * 512 * 512 * 512


def tile_attend_tab_twosum_bestruns_pl_kernel(
    tc, keys_words, keys_scales, notes, more_words, more_scales, users2, rowf, vals,
    offs, offs2, offs3, offs4, out_0, out_1, out_2,
):
    nc = tc.nc
    with ExitStack() as ctx:
        held = ctx.enter_context(tc.tile_pool(name="held", bufs=1))
        psum = ctx.enter_context(tc.psum_pool(name="psum", bufs=1))

        def sb(name, shape, dtype):
            return held.tile(shape, dtype, name=name, align_bytes=64)

        def load_list(name, dram):
            tile = held.tile([P, SLOTS // 16], U16, name=name)
            nc.sync.dma_start(tile[:], dram)
            return tile

        def load_plane(name, dram, t):
            tile = sb(f"{name}{t}", [P, dram.shape[1]], F32)
            nc.sync.dma_start(tile[:], dram.rearrange("(p t) c -> t p c", t=PACK)[t])
            return tile

        def load_words(name, dram):
            tile = sb(name, [P, dram.shape[2] // 2], U16)
            nc.sync.dma_start(tile[:].bitcast(I32), dram[0].bitcast(I32))
            return tile

        def zeroed(name, width):
            tile = sb(name, [P, width], U8)
            nc.gpsimd.memset(tile[:].bitcast(I32), 0)
            return tile

        def load_scale_rows(tile, dram, q):
            nc.sync.dma_start(
                tile[32 * q : 32 * q + 4, :].bitcast(I32), dram[0, 4 * q : 4 * q + 4, :].bitcast(I32)
            )

        keys_scale_pool = zeroed("keys_scale_pool", keys_scales.shape[2])
        more_scale_pool = zeroed("more_scale_pool", more_scales.shape[2])

        token_list = load_list("token_list", offs)
        keys_pool = load_words("keys_pool", keys_words)
        load_scale_rows(keys_scale_pool, keys_scales, 0)
        note_list = load_list("note_list", offs2)
        note_planes = [load_plane("note_plane", notes, 0)]
        load_scale_rows(keys_scale_pool, keys_scales, 1)
        load_scale_rows(keys_scale_pool, keys_scales, 2)
        note_planes.append(load_plane("note_plane", notes, 1))
        load_scale_rows(keys_scale_pool, keys_scales, 3)
        more_list = load_list("more_list", offs3)
        more_pool = load_words("more_pool", more_words)
        note_planes.append(load_plane("note_plane", notes, 2))
        load_scale_rows(more_scale_pool, more_scales, 0)
        load_scale_rows(more_scale_pool, more_scales, 1)
        note_planes.append(load_plane("note_plane", notes, 3))
        load_scale_rows(more_scale_pool, more_scales, 2)
        load_scale_rows(more_scale_pool, more_scales, 3)
        user_list = load_list("user_list", offs4)
        user_planes = [load_plane("user_plane", users2, t) for t in range(PACK)]
        row_factor = sb("row_factor", [P, PACK], F32)
        nc.sync.dma_start(row_factor[:], rowf.rearrange("(p t) o -> p (t o)", t=PACK))
        value_planes = [load_plane("value_plane", vals, t) for t in range(PACK)]

        identity = sb("identity", [P, P], F32)
        make_identity(nc, identity[:])

        def gather_words(name, pool, offsets):
            words = sb(f"{name}_words", [P, SLOTS], U16)
            nc.vector.tensor_copy(words[:], pool[:].indirect(offsets[:]))
            dealt = sb(f"{name}_dealt", [P, SLOTS], U16)
            nc.vector.tensor_copy(
                dealt[:].rearrange("p (r s) -> p r s", r=PACK), words[:].rearrange("p (s r) -> p r s", r=PACK)
            )
            return dealt

        def gather_scales(name, pool, offsets):
            scales = sb(f"{name}_scales", [P, SLOTS], U8)
            nc.vector.tensor_copy(scales[:].rearrange("p (r s) -> p s r", r=PACK), pool[:].indirect(offsets[:]))
            return scales

        def half_of(offsets, h):
            return offsets[:, h * 16 : (h + 1) * 16]

        def weave(name, picked):
            woven = sb(name, [P, picked.shape[2], PACK], BF16)
            nc.vector.tensor_copy(woven[:], picked.rearrange("p t j -> p j t"))
            return woven

        def quantize(name, woven, width):
            codes = sb(f"{name}_codes", [P, width], U32)
            scales = sb(f"{name}_scales", [P, width], U8)
            nc.vector.quantize_mx(
                out=codes[:].bitcast(FP8X4), scales=scales[:], in_=woven[:].rearrange("p j t -> p (j t)")
            )
            return codes, scales

        notes_picked = sb("notes_picked", [P, PACK, SLOTS], BF16)
        users_picked = sb("users_picked", [P, PACK, SLOTS], BF16)
        keys_dealt = gather_words("keys", keys_pool, token_list)
        keys_dealt_scales = gather_scales("keys", keys_scale_pool, token_list)
        more_dealt = gather_words("more", more_pool, more_list)
        for t in range(PACK - 1):
            nc.scalar.activation(notes_picked[:, t, :], note_planes[t][:].indirect(note_list[:]), COPY)
        nc.vector.tensor_copy(notes_picked[:, PACK - 1, :], note_planes[PACK - 1][:].indirect(note_list[:]))
        more_dealt_scales = gather_scales("more", more_scale_pool, more_list)
        notes_codes, notes_scales = quantize("notes", weave("notes_woven", notes_picked[:]), SLOTS)

        for t in range(2):
            nc.scalar.activation(users_picked[:, t, :], user_planes[t][:].indirect(user_list[:]), COPY)
        for t, h in ((2, 0), (2, 1), (3, 1)):
            nc.scalar.activation(
                users_picked[:, t, h * HALF : (h + 1) * HALF],
                user_planes[t][:].indirect(half_of(user_list, h)),
                COPY,
            )
        nc.vector.tensor_copy(users_picked[:, 3, :HALF], user_planes[3][:].indirect(half_of(user_list, 0)))

        banks = [psum.tile([P, PACK, CHUNK], F32, name=f"bank{c}") for c in range(CHUNKS)]

        def table_passes(c, words, scales, moving_codes, moving_scales, opens):
            for t in range(PACK):
                rows = slice(t * P, (t + 1) * P)
                nc.tensor.matmul_mx(
                    out=banks[c][:, t, :],
                    lhsT=words[:, rows].bitcast(FP4X4),
                    lhsT_scale=scales[:, rows],
                    rhs=moving_codes.bitcast(FP8X4),
                    rhs_scale=moving_scales,
                    start=opens and t == 0,
                    stop=not opens and t == PACK - 1,
                )

        for c in range(CHUNKS):
            cols = slice(c * CHUNK, (c + 1) * CHUNK)
            table_passes(c, keys_dealt, keys_dealt_scales, notes_codes[:, cols], notes_scales[:, cols], True)

        table_codes = sb("table_codes", [P, SLOTS], U32)
        table_scales = sb("table_scales", [P, SLOTS], U8)
        factor = row_factor[:].unsqueeze(1).to_broadcast([P, CHUNK, PACK])
        table_woven = [sb(f"table_woven{h}", [P, HALF, PACK], BF16) for h in range(2)]
        for h in range(2):
            users_woven = weave(f"users_woven{h}", users_picked[:, :, h * HALF : (h + 1) * HALF])
            codes, scales = quantize(f"users{h}", users_woven, HALF)
            for k in range(2):
                cols = slice(k * CHUNK, (k + 1) * CHUNK)
                table_passes(2 * h + k, more_dealt, more_dealt_scales, codes[:, cols], scales[:, cols], False)
        for h in range(2):
            for k in range(2):
                nc.vector.tensor_tensor(
                    table_woven[h][:, k * CHUNK : (k + 1) * CHUNK, :],
                    banks[2 * h + k][:].rearrange("p t j -> p j t"),
                    factor,
                    mybir.AluOpType.mult,
                )
        for h in range(2):
            cols = slice(h * HALF, (h + 1) * HALF)
            nc.vector.quantize_mx(
                out=table_codes[:, cols].bitcast(FP8X4),
                scales=table_scales[:, cols],
                in_=table_woven[h][:].rearrange("p j t -> p (j t)"),
            )

        def pick_and_turn(t):
            picked = sb(f"values_picked{t}", [P, SLOTS], BF16)
            if t + 1 < PACK:
                nc.scalar.activation(picked[:], value_planes[t][:].indirect(token_list[:]), COPY)
            else:
                nc.scalar.activation(picked[:, :HALF], value_planes[t][:].indirect(half_of(token_list, 0)), COPY)
                nc.vector.tensor_copy(picked[:, HALF:], value_planes[t][:].indirect(half_of(token_list, 1)))
            pairs = picked[:].bitcast(F32)
            turned = psum.tile([P, 2, P], F32, name=f"turned{t}")
            for u in range(2):
                nc.tensor.transpose(turned[:, u, :], pairs[:, u::2], identity[:])
            return turned

        def weave_turned(slot, turned):
            woven = sb(slot, [P, P, PACK], BF16)
            nc.scalar.copy(
                woven[:].rearrange("p e t -> p (e t)").bitcast(F32).rearrange("p (e u) -> p e u", u=2),
                turned[:].rearrange("p u e -> p e u"),
            )
            return woven

        def multiply(t, woven, bank):
            codes, scales = quantize(f"values{t}", woven, P)
            sums = psum.tile([P, SLOTS], F32, name=bank)
            nc.tensor.matmul_mx(
                out=sums[:],
                lhsT=codes[:].bitcast(FP8X4),
                lhsT_scale=scales[:],
                rhs=table_codes[:].bitcast(FP8X4),
                rhs_scale=table_scales[:],
                start=True,
                stop=True,
            )
            return sums

        def best_of_runs(best, sums):
            nc.vector.tensor_reduce(
                best, sums[:].rearrange("p (n k) -> p n k", k=RUN), mybir.AxisListType.X, mybir.AluOpType.max
            )

        out_pairs = out_0.rearrange("(p u e) n -> u p e n", u=2, e=2)
        best_pairs = []
        for u in range(2):
            even, odd = 2 * u, 2 * u + 1
            turned = [pick_and_turn(even), pick_and_turn(odd)]
            woven = [weave_turned(f"value_plane{odd}", turned[0]), weave_turned(f"values_woven{odd}", turned[1])]
            sums = [multiply(2 * u + e, woven[e], f"bank{2 * u + e}") for e in range(2)]
            best = sb(f"best{u}", [P, 2, RUNS], F32)
            for e in range(2):
                best_of_runs(best[:, e, :], sums[e])
            nc.sync.dma_start(out_pairs[u], best[:])
            best_pairs.append(best)

        best_woven = sb("values_picked3", [P, RUNS, PACK], BF16)
        for u, best in enumerate(best_pairs):
            nc.scalar.copy(best_woven[:, :, 2 * u : 2 * u + 2], best[:].rearrange("p e n -> p n e"))
        best_codes, best_scales = quantize("best", best_woven, RUNS)
        nc.sync.dma_start(
            out_1[0].rearrange("p c r -> p (c r)").bitcast(I32), best_codes[:].bitcast(I32)
        )
        for q in range(4):
            queue = nc.scalar if q % 2 == 0 else nc.sync
            queue.dma_start(
                out_2[0, 4 * q : 4 * q + 4, :].bitcast(I32), best_scales[32 * q : 32 * q + 4, :].bitcast(I32)
            )
